import numpy as np
import ml_dtypes


def mxq(x, axis, fmt="e4m3"):
    dtype, down = {"e4m3": (ml_dtypes.float8_e4m3fn, 7), "e5m2": (ml_dtypes.float8_e5m2, 14)}[fmt]
    v = np.moveaxis(np.asarray(x, np.float32).astype(ml_dtypes.bfloat16).astype(np.float64), axis, -1)
    blocks = v.reshape(v.shape[:-1] + (-1, 32))
    amax = np.abs(blocks).max(-1, keepdims=True)
    byte = np.maximum(np.where(amax > 0, np.frexp(amax)[1] - 1 + 127, 0) - down, 1)
    scale = np.exp2(byte - 127.0)
    codes = (blocks / scale).astype(np.float32).astype(dtype).astype(np.float64)
    return np.moveaxis((codes * scale).reshape(v.shape), -1, axis)


WIDE = False


def mx_kscale(k):
    if not WIDE:
        return np.ones(k)
    levels = np.array([10, -10, 5, -5, 0])
    if k % 512:
        return np.exp2(np.random.permutation(np.resize(levels, k // 32))).repeat(32)
    a = np.empty((k // 512, 16))
    for p in range(k // 512):
        a[p, :8] = np.random.permutation(np.resize(levels, 8))
        for g in range(8):
            far = levels[np.abs(levels - a[p, g]) >= 10]
            a[p, g + 8] = far[np.random.randint(len(far))]
    return np.exp2(a.ravel()).repeat(32)


def f64(x):
    return np.asarray(x).astype(np.float64)


def striped(idx):
    return np.tile(idx.reshape(-1, 16).T, (8, 1)).astype(np.uint16)


def unstriped(offs):
    return offs[:16].T.reshape(-1).astype(np.int64)


E2M1 = np.array([0.0, 0.5, 1.0, 1.5, 2.0, 3.0, 4.0, 6.0, -0.0, -0.5, -1.0, -1.5, -2.0, -3.0, -4.0, -6.0])


def pack_weight(w, fmt):
    k, n = w.shape
    w = f64(np.asarray(w, np.float32).astype(ml_dtypes.bfloat16)).reshape(k // 32, 32, n)
    amax = np.abs(w).max(1)
    if fmt == "e4m3":
        byte = np.frexp(amax)[1] - 1 + 127 - 7
    else:
        mant, ex = np.frexp(amax / 6.0)
        byte = np.where(mant > 0.5, ex, ex - 1) + 127
    byte = np.clip(np.where(amax > 0, byte, 1), 1, 254)
    scaled = (w * np.exp2(127.0 - byte)[:, None, :]).reshape(k, n).astype(np.float32)
    by_word = np.ascontiguousarray(scaled.reshape(k // 512, 128, 4, n).transpose(0, 1, 3, 2))
    if fmt == "e4m3":
        words = by_word.astype(ml_dtypes.float8_e4m3fn).view(np.uint8)
    else:
        c = by_word.astype(ml_dtypes.float4_e2m1fn).view(np.uint8) & 0xF
        words = (c[..., 0::2] | (c[..., 1::2] << 4)).reshape(k // 512, 128, 2 * n)
    return np.ascontiguousarray(words), np.ascontiguousarray(byte.astype(np.uint8).reshape(k // 512, 16, n))


def unpack_weight(words, scales, fmt):
    g, _, n = scales.shape
    words = np.ascontiguousarray(words).reshape(g, 128, n, -1)
    if fmt == "e4m3":
        vals = words.view(ml_dtypes.float8_e4m3fn).astype(np.float64)
    else:
        nib = np.empty((g, 128, n, 4), np.uint8)
        nib[..., 0::2] = words & 0xF
        nib[..., 1::2] = words >> 4
        vals = E2M1[nib]
    vals = vals * np.repeat(np.exp2(scales.astype(np.float64) - 127.0), 8, axis=1)[..., None]
    return vals.transpose(0, 1, 3, 2).reshape(g * 512, n)


def gelu(v):
    return 0.5 * v * (1.0 + np.tanh(np.sqrt(2.0 / np.pi) * (v + 0.044715 * v**3)))


def bf(x):
    return np.asarray(x, np.float32).astype(ml_dtypes.bfloat16)


def planes(Y):
    n, m = Y.shape
    b = f64(bf(Y)).reshape(n // 32, 32, m)
    amax = np.abs(b).max(1)
    byte = np.clip(np.where(amax > 0, np.frexp(amax)[1] - 1 + 127 - 7, 1), 1, 254)
    codes = (b * np.exp2(127.0 - byte)[:, None, :]).reshape(n, m).astype(np.float32).astype(ml_dtypes.float8_e4m3fn).view(np.uint8)
    words = codes.reshape(n // 512, 128, 4, m).transpose(0, 1, 3, 2)
    return np.ascontiguousarray(words), np.ascontiguousarray(byte.astype(np.uint8).reshape(n // 512, 16, m))


K, H, N, T, S, P = 1024, 512, 512, 4096, 1024, 512

def setup_inputs():
    n = np.random.standard_normal
    s = mx_kscale(K)[:, None]
    u = mx_kscale(H)[:, None]
    col = np.exp(0.4 * n(N))[None, :]
    perm = np.random.permutation(S)
    d = {}
    d["tab_words"], d["tab_scales"] = pack_weight(n((K, T)) * s, "e4m3")
    d["offs"] = striped(np.random.permutation(T)[:S])
    d["pos1"] = striped(perm[:P])
    d["pos2"] = striped(perm[S - P:])
    d["w1"] = (1.8 * n((K, H)) / K ** 0.5 / s).astype(np.float32)
    d["w2_words"], d["w2_scales"] = pack_weight(n((K, H)) / K ** 0.5 / s, "e2m1")
    d["gain"] = (np.exp(0.3 * n(H)) * u[:, 0]).astype(np.float32)
    d["w3"] = (n((H, N)) / H ** 0.5 / u * col).astype(np.float32)
    d["w4_words"], d["w4_scales"] = pack_weight(0.7 * n((K, N)) / K ** 0.5 / s * col, "e4m3")
    d["trust"] = n((N, S)).astype(np.float32)
    return d

def reference(tab_words, tab_scales, offs, pos1, pos2, w1, w2_words, w2_scales, gain, w3, w4_words, w4_scales, trust):
    v = unpack_weight(tab_words, tab_scales, "e4m3")[:, unstriped(offs)]
    w2 = unpack_weight(w2_words, w2_scales, "e2m1")
    w4 = unpack_weight(w4_words, w4_scales, "e4m3")
    bounded = np.tanh(mxq(f64(w1), 0, "e4m3").T @ v)
    linear = w2.T @ v
    h = np.minimum(bounded, linear) * f64(gain)[:, None]
    deep = mxq(f64(w3), 0, "e4m3").T @ mxq(h, 0, "e4m3")
    skip = w4.T @ v
    g2 = deep - f64(trust) * skip
    diff = g2[:, unstriped(pos1)] - g2[:, unstriped(pos2)]
    y = np.square(diff)
    words, scales = planes(y)
    return y, words, scales

@@ -1,0 +1,292 @@
+from contextlib import ExitStack
+
+import concourse.mybir as mybir
+from concourse.masks import make_identity
+
+K, H, N, T, S, M = 1024, 512, 512, 4096, 1024, 512
+FLOPS = 2 * S * (K * H + K * H + K * N + H * N)
+
+F32 = mybir.dt.float32
+BF16 = mybir.dt.bfloat16
+I32 = mybir.dt.int32
+U32 = mybir.dt.uint32
+U16 = mybir.dt.uint16
+U8 = mybir.dt.uint8
+FP8X4 = mybir.dt.float8_e4m3fn_x4
+FP4X4 = mybir.dt.float4_e2m1fn_x4
+ALU = mybir.AluOpType
+ACT = mybir.ActivationFunctionType
+
+P = 128
+PACK = 4
+PASSES = K // (P * PACK)
+QUADS = 4
+HALF = 512
+CHUNK = 256
+LANES = 16
+
+
+def tile_list_boundary_marker_discrepancy_kernel(
+    tc, tab_words, tab_scales, offs, pos1, pos2, w1, w2_words, w2_scales, gain, w3, w4_words, w4_scales, trust,
+    out_0, out_1, out_2,
+):
+    nc = tc.nc
+    with ExitStack() as ctx:
+        lists = ctx.enter_context(tc.tile_pool(name="lists", bufs=1))
+        keep = ctx.enter_context(tc.tile_pool(name="keep", bufs=1))
+        ring = ctx.enter_context(tc.tile_pool(name="ring", bufs=2))
+        psum = ctx.enter_context(tc.psum_pool(name="psum", bufs=1))
+
+        def held(shape, dtype, name):
+            return keep.tile(shape, dtype, name=name, align_bytes=64)
+
+        offs_sb = lists.tile([P, S // LANES], U16, name="offs_sb")
+        pos1_sb = lists.tile([P, M // LANES], U16, name="pos1_sb")
+        pos2_sb = lists.tile([P, M // LANES], U16, name="pos2_sb")
+
+        def shared(shape, dtype, name, tag):
+            return keep.tile(shape, dtype, name=name, tag=tag, align_bytes=64)
+
+        nc.sync.dma_start(offs_sb[:], offs)
+        tab_sc = shared([P, T], U8, "tab_sc", "third")
+        nc.sync.dma_start(out=tab_sc[0:32, :].bitcast(I32), in_=tab_scales.rearrange("a q t -> (a q) t").bitcast(I32))
+        nc.vector.memset(tab_sc[32:64, :].bitcast(I32), 0)
+        nc.gpsimd.memset(tab_sc[64:P, :].bitcast(I32), 0)
+        tab_w = [shared([P, T], U32, "tab_w%d" % a, ("first", "second")[a]) for a in range(PASSES)]
+
+        def load_tab(a):
+            nc.sync.dma_start(out=tab_w[a][:].bitcast(I32), in_=tab_words[a].rearrange("p t i -> p (t i)").bitcast(I32))
+
+        load_tab(0)
+        nc.sync.dma_start(pos1_sb[:], pos1)
+        nc.sync.dma_start(pos2_sb[:], pos2)
+        w4_raw = held([P, PASSES * N], I32, "w4_raw")
+        nc.sync.dma_start(out=w4_raw[:].rearrange("p (a c) -> p a c", a=PASSES),
+                          in_=w4_words.rearrange("a p c i -> p a (c i)").bitcast(I32))
+        load_tab(1)
+
+        ident = held([P, P], F32, "ident")
+        make_identity(nc, ident[:])
+        w4s_raw = held([P, N], U8, "w4s_raw")
+        nc.gpsimd.memset(w4s_raw[:].bitcast(I32), 0)
+        for q in range(QUADS):
+            nc.gpsimd.dma_start(out=w4s_raw[32 * q : 32 * q + 8, :].bitcast(I32),
+                                in_=w4_scales[:, 4 * q : 4 * q + 4, :].bitcast(I32))
+        gain_rows = held([P, P], F32, "gain_rows")
+        nc.vector.memset(gain_rows[:], 0.0)
+        nc.gpsimd.dma_start(out=gain_rows[0:PACK, :].rearrange("t (q i) -> t q i", i=8),
+                            in_=gain.rearrange("(q t i) -> t q i", t=PACK, i=8))
+        w2s_raw = held([P, PASSES * H // 4], I32, "w2s_raw")
+        nc.gpsimd.memset(w2s_raw[:], 0)
+        for q in range(QUADS):
+            nc.gpsimd.dma_start(out=w2s_raw[32 * q : 32 * q + 4, :].rearrange("r (a c) -> r a c", a=PASSES),
+                                in_=w2_scales[:, 4 * q : 4 * q + 4, :].bitcast(I32).rearrange("a r c -> r a c"))
+        v_s = [held([P, S], U8, "v_s%d" % a) for a in range(PASSES)]
+        for a in range(PASSES):
+            nc.vector.memset(v_s[a][:].bitcast(I32), 0)
+        gain_ps = psum.tile([P, P], F32, name="gain_ps")
+        nc.tensor.transpose(gain_ps[:], gain_rows[:], ident[:])
+
+        v_w = [held([P, S], U32, "v_w%d" % a) for a in range(PASSES)]
+        v_sc = held([P, S], U8, "v_sc")
+
+        def gather_words(a):
+            for b in range(2):
+                nc.vector.tensor_copy(v_w[a][:, b * HALF : (b + 1) * HALF],
+                                      tab_w[a][:].indirect(offs_sb[:, b * HALF // LANES : (b + 1) * HALF // LANES]))
+
+        nc.vector.tensor_copy(v_sc[:], tab_sc[:].indirect(offs_sb[:]))
+        for a in range(PASSES):
+            for q in range(QUADS):
+                row = 16 * a + 4 * q
+                nc.scalar.dma_start(out=v_s[a][32 * q : 32 * q + 4, :].bitcast(I32), in_=v_sc[row : row + 4, :].bitcast(I32))
+        w2_raw = shared([P, PASSES * H // 2], I32, "w2_raw", "third")
+        nc.sync.dma_start(out=w2_raw[:].rearrange("p (a c) -> p a c", a=PASSES),
+                          in_=w2_words.rearrange("a p c -> p a c").bitcast(I32))
+        gather_words(0)
+        w1_both = shared([P, PASSES, PACK, H], F32, "w1_both", "first")
+        w1_raw = [w1_both[:, a] for a in range(PASSES)]
+        for a in range(PASSES):
+            nc.sync.dma_start(out=w1_raw[a], in_=w1[512 * a : 512 * (a + 1), :].rearrange("(p j) c -> p j c", j=PACK))
+        w4_q = held([P, PASSES * N], I32, "w4_q")
+        nc.vector.tensor_copy(w4_q[:].rearrange("p (a t m i) -> p a m t i", a=PASSES, t=PACK, i=4),
+                              w4_raw[:].rearrange("p (a m i t) -> p a m t i", a=PASSES, t=PACK, i=4))
+        w4_s = held([P, N], U8, "w4_s")
+        nc.vector.tensor_copy(w4_s[:].rearrange("p (t m) -> p t m", t=PACK), w4s_raw[:].rearrange("p (m t) -> p t m", t=PACK))
+        gather_words(1)
+        late = shared([P, 2, PACK, HALF], F32, "late", "second")
+        trust_sb = [late[:, 0]]
+        w3_raw = late[:, 1]
+        trust_rows = trust.rearrange("(p t) j -> p t j", t=PACK)
+        nc.sync.dma_start(out=trust_sb[0], in_=trust_rows[:, :, 0:HALF])
+        w3_rows = w3.rearrange("(q s i) n -> s q i n", s=PACK, i=8)
+        for s in range(PACK):
+            nc.sync.dma_start(out=w3_raw[:, s, :], in_=w3_rows[s])
+        w2_q = held([P, PASSES * H * 2], U8, "w2_q")
+        nc.vector.tensor_copy(w2_q[:].bitcast(I32).rearrange("p (a t q i) -> p a t q i", a=PASSES, t=PACK, i=4),
+                              w2_raw[:].rearrange("p (a q t i) -> p a t q i", a=PASSES, t=PACK, i=4))
+        w2_s = held([P, PASSES * H], U8, "w2_s")
+        nc.vector.tensor_copy(w2_s[:].bitcast(I32).rearrange("p (a t q i) -> p a t q i", a=PASSES, t=PACK, i=2),
+                              w2s_raw[:].rearrange("p (a q t i) -> p a t q i", a=PASSES, t=PACK, i=2))
+
+        skip = [held([P, PACK, HALF], F32, "skip%d" % b) for b in range(2)]
+        for b in range(2):
+            cols = slice(b * HALF, (b + 1) * HALF)
+            for t in range(PACK):
+                bank = psum.tile([P, HALF], F32, name="wide", bufs=2)
+                for a in range(PASSES):
+                    nc.tensor.matmul_mx(out=bank[:], lhsT=w4_q[:, a * N + t * P : a * N + (t + 1) * P].bitcast(FP8X4),
+                                        lhsT_scale=w4_s[4 * a : P, t * P : (t + 1) * P],
+                                        rhs=v_w[a][:, cols].bitcast(FP8X4), rhs_scale=v_s[a][:, cols],
+                                        start=(a == 0), stop=(a == PASSES - 1))
+                nc.scalar.activation(out=skip[b][:, t, :], in_=bank[:], func=ACT.Copy)
+
+        w1_q = {}
+        w1_s = {}
+        for a in range(PASSES):
+            grouped = []
+            for u in range(2):
+                g = held([P, 2 * P * PACK], BF16, "w1_g%d%d" % (a, u))
+                nc.vector.tensor_copy(
+                    g[:].rearrange("p (e q i j) -> p e q j i", e=2, i=8, j=PACK),
+                    w1_raw[a].rearrange("p j (q t i) -> p t q j i", t=PACK, i=8)[:, 2 * u : 2 * u + 2])
+                grouped.append(g)
+            for u in range(2):
+                w1_q[a, u] = held([P, 2 * P], U32, "w1_q%d%d" % (a, u))
+                w1_s[a, u] = held([P, 2 * P], U8, "w1_s%d%d" % (a, u))
+                nc.vector.quantize_mx(out=w1_q[a, u][:].bitcast(FP8X4), scales=w1_s[a, u][:], in_=grouped[u][:])
+
+        trust_sb.append(shared([P, PACK, HALF], F32, "trust_late", "first")[:])
+        nc.sync.dma_start(out=trust_sb[1], in_=trust_rows[:, :, HALF:S])
+
+        h_q = [held([P, HALF], U32, "h_q%d" % b) for b in range(2)]
+        h_s = [held([P, HALF], U8, "h_s%d" % b) for b in range(2)]
+        gain_tn = gain_ps[:, 0:PACK].unsqueeze(1).unsqueeze(3).to_broadcast([P, CHUNK // 2, PACK, 2])
+        lesser = {}
+        h_bf = {}
+
+        def products(c):
+            cols = slice(c * CHUNK, (c + 1) * CHUNK)
+            lesser[c] = ring.tile([P, PACK * CHUNK], F32, name="lesser")
+            for u in range(2):
+                lin = psum.tile([P, 2, CHUNK], F32, name="lin", bufs=3)
+                for e in range(2):
+                    t = 2 * u + e
+                    for a in range(PASSES):
+                        nc.tensor.matmul_mx(out=lin[:, e, :],
+                                            lhsT=w2_q[:, 2 * (a * H + t * P) : 2 * (a * H + (t + 1) * P)].bitcast(FP4X4),
+                                            lhsT_scale=w2_s[:, a * H + t * P : a * H + (t + 1) * P],
+                                            rhs=v_w[a][:, cols].bitcast(FP8X4), rhs_scale=v_s[a][:, cols],
+                                            start=(a == 0), stop=(a == PASSES - 1))
+                pre = psum.tile([P, 2, CHUNK], F32, name="pre", bufs=2)
+                for a in range(PASSES):
+                    for e in range(2):
+                        nc.tensor.matmul_mx(out=pre[:, e, :], lhsT=w1_q[a, u][:, e * P : (e + 1) * P].bitcast(FP8X4),
+                                            lhsT_scale=w1_s[a, u][:, e * P : (e + 1) * P],
+                                            rhs=v_w[a][:, cols].bitcast(FP8X4), rhs_scale=v_s[a][:, cols],
+                                            start=(a == 0 and e == 0), stop=(a == PASSES - 1 and e == 1))
+                bounded = ring.tile([P, 2 * CHUNK], F32, name="bounded", bufs=3)
+                nc.scalar.activation(out=bounded[:], in_=pre[:].rearrange("p e n -> p (e n)"), func=ACT.Tanh)
+                nc.vector.tensor_tensor(lesser[c][:, 2 * u * CHUNK : 2 * (u + 1) * CHUNK],
+                                        lin[:].rearrange("p e n -> p (e n)"), bounded[:], ALU.min)
+
+        def apply_gain(c):
+            h_bf[c] = ring.tile([P, CHUNK * PACK], BF16, name="h_bf", align_bytes=64)
+            nc.vector.tensor_tensor(h_bf[c][:].rearrange("p (c i t) -> p c t i", i=2, t=PACK),
+                                    lesser[c][:].rearrange("p (t c i) -> p c t i", i=2, t=PACK), gain_tn, ALU.mult)
+
+        def quantise_h(c):
+            cols = slice((c % 2) * CHUNK, (c % 2 + 1) * CHUNK)
+            nc.vector.quantize_mx(out=h_q[c // 2][:, cols].bitcast(FP8X4), scales=h_s[c // 2][:, cols], in_=h_bf[c][:])
+
+        def weigh_skip(b):
+            for t in range(PACK):
+                nc.vector.tensor_tensor(skip[b][:, t, :], skip[b][:, t, :], trust_sb[b][:, t, :], ALU.mult)
+
+        w3_g = held([P, N * PACK], BF16, "w3_g")
+        w3_q = held([P, N], U32, "w3_q")
+        w3_s = held([P, N], U8, "w3_s")
+
+        def round_w3(part):
+            ms = slice(32 * part, 32 * (part + 1))
+            nc.scalar.activation(out=w3_g[:].rearrange("p (t m s) -> p m s t", t=PACK, s=PACK)[:, ms],
+                                 in_=w3_raw.rearrange("p s (m t) -> p m s t", t=PACK)[:, ms], func=ACT.Copy)
+
+        chunks = S // CHUNK
+        for c in range(chunks):
+            products(c)
+            if c > 0:
+                quantise_h(c - 1)
+            apply_gain(c)
+            if c >= 2:
+                round_w3(2 * (c - 2))
+                round_w3(2 * (c - 2) + 1)
+        weigh_skip(0)
+        quantise_h(chunks - 1)
+        nc.vector.quantize_mx(out=w3_q[:].bitcast(FP8X4), scales=w3_s[:], in_=w3_g[:])
+        weigh_skip(1)
+
+        g2 = [held([P, S], F32, "g2_%d" % t) for t in range(PACK)]
+        y = held([P, PACK, M], F32, "y")
+        y_rows = out_0.rearrange("(p t) m -> p t m", t=PACK)
+        first = {}
+
+        def second_stage(t, b):
+            bank = psum.tile([P, HALF], F32, name="wide", bufs=2)
+            nc.tensor.matmul_mx(out=bank[:], lhsT=w3_q[:, t * P : (t + 1) * P].bitcast(FP8X4),
+                                lhsT_scale=w3_s[:, t * P : (t + 1) * P],
+                                rhs=h_q[b][:].bitcast(FP8X4), rhs_scale=h_s[b][:], start=True, stop=True)
+            nc.vector.tensor_tensor(g2[t][:, b * HALF : (b + 1) * HALF], bank[:], skip[b][:, t, :], ALU.subtract)
+
+        def pick_first(t, lo, hi):
+            first[t, lo] = ring.tile([P, M], F32, name="first", bufs=3)
+            nc.vector.tensor_copy(first[t, lo][:, 0 : hi - lo], g2[t][:].indirect(pos1_sb[:, lo // LANES : hi // LANES]))
+
+        def pick_second(t, lo, hi):
+            diff = ring.tile([P, M], F32, name="diff", bufs=3)
+            nc.vector.tensor_tensor(diff[:, 0 : hi - lo], g2[t][:].indirect(pos2_sb[:, lo // LANES : hi // LANES]),
+                                    first[t, lo][:, 0 : hi - lo], ALU.subtract)
+            nc.scalar.activation(out=y[:, t, lo:hi], in_=diff[:, 0 : hi - lo], func=ACT.Square)
+            nc.sync.dma_start(out=y_rows[:, t, lo:hi], in_=y[:, t, lo:hi])
+
+        y_q = held([P, M], U32, "y_q")
+        y_s = held([P, M], U8, "y_s")
+        y_bf = [held([P, M // 2 * PACK], BF16, "y_bf%d" % b) for b in range(2)]
+        words_out = out_1[0].rearrange("p m t -> p (m t)").bitcast(I32)
+        mid = M // 2
+
+        def planes(b):
+            cols = slice(b * mid, (b + 1) * mid)
+            nc.vector.quantize_mx(out=y_q[:, cols].bitcast(FP8X4), scales=y_s[:, cols], in_=y_bf[b][:])
+            nc.sync.dma_start(out=words_out[:, cols], in_=y_q[:, cols].bitcast(I32))
+
+        def y_views(b):
+            return (y_bf[b][:].rearrange("p (c i t) -> p c t i", i=2, t=PACK),
+                    y[:, :, b * mid : (b + 1) * mid].rearrange("p t (c i) -> p c t i", i=2))
+
+        second_stage(0, 0)
+        second_stage(0, 1)
+        for t in range(2):
+            second_stage(t + 1, 0)
+            pick_first(t, 0, M)
+            second_stage(t + 1, 1)
+            pick_second(t, 0, M)
+        second_stage(3, 0)
+        pick_first(2, 0, mid)
+        second_stage(3, 1)
+        pick_second(2, 0, mid)
+        pick_first(3, 0, mid)
+        pick_first(2, mid, M)
+        pick_second(3, 0, mid)
+        dst, src = y_views(0)
+        nc.scalar.activation(out=dst, in_=src, func=ACT.Copy)
+        pick_first(3, mid, M)
+        pick_second(2, mid, M)
+        pick_second(3, mid, M)
+        planes(0)
+        dst, src = y_views(1)
+        nc.vector.tensor_copy(dst, src)
+        planes(1)
+        for q in range(QUADS):
+            eng = (nc.sync, nc.scalar)[q % 2]
+            eng.dma_start(out=out_2[0, 4 * q : 4 * q + 4, :].bitcast(I32), in_=y_s[32 * q : 32 * q + 4, :].bitcast(I32))

@@ -24,6 +24,8 @@ QUADS = 4
 HALF = 512
 CHUNK = 256
 LANES = 16
+KB = 1024
+BANKS = 7
 
 
 def tile_list_boundary_marker_discrepancy_kernel(
@@ -34,6 +36,7 @@ def tile_list_boundary_marker_discrepancy_kernel(
     with ExitStack() as ctx:
         lists = ctx.enter_context(tc.tile_pool(name="lists", bufs=1))
         keep = ctx.enter_context(tc.tile_pool(name="keep", bufs=1))
+        stage = ctx.enter_context(tc.tile_pool(name="stage", bufs=1))
         ring = ctx.enter_context(tc.tile_pool(name="ring", bufs=2))
         psum = ctx.enter_context(tc.psum_pool(name="psum", bufs=1))
 
@@ -44,46 +47,40 @@ def tile_list_boundary_marker_discrepancy_kernel(
         pos1_sb = lists.tile([P, M // LANES], U16, name="pos1_sb")
         pos2_sb = lists.tile([P, M // LANES], U16, name="pos2_sb")
 
-        def shared(shape, dtype, name, tag):
-            return keep.tile(shape, dtype, name=name, tag=tag, align_bytes=64)
+        def staged(shape, dtype, name, offset):
+            return stage.tile(shape, dtype, name=name, align_bytes=64, offset=offset)
 
         nc.sync.dma_start(offs_sb[:], offs)
-        tab_sc = shared([P, T], U8, "tab_sc", "third")
+        tab_sc = staged([P, T], U8, "tab_sc", 31 * KB + KB // 2)
         nc.sync.dma_start(out=tab_sc[0:32, :].bitcast(I32), in_=tab_scales.rearrange("a q t -> (a q) t").bitcast(I32))
-        nc.vector.memset(tab_sc[32:64, :].bitcast(I32), 0)
-        nc.gpsimd.memset(tab_sc[64:P, :].bitcast(I32), 0)
-        tab_w = [shared([P, T], U32, "tab_w%d" % a, ("first", "second")[a]) for a in range(PASSES)]
+        nc.sync.dma_start(pos1_sb[:], pos1)
+        nc.sync.dma_start(pos2_sb[:], pos2)
+        tab_w = {}
 
         def load_tab(a):
+            tab_w[a] = staged([P, T], U32, "tab_w%d" % a, 16 * KB * a)
             nc.sync.dma_start(out=tab_w[a][:].bitcast(I32), in_=tab_words[a].rearrange("p t i -> p (t i)").bitcast(I32))
 
         load_tab(0)
-        nc.sync.dma_start(pos1_sb[:], pos1)
-        nc.sync.dma_start(pos2_sb[:], pos2)
         w4_raw = held([P, PASSES * N], I32, "w4_raw")
         nc.sync.dma_start(out=w4_raw[:].rearrange("p (a c) -> p a c", a=PASSES),
                           in_=w4_words.rearrange("a p c i -> p a (c i)").bitcast(I32))
-        load_tab(1)
-
-        ident = held([P, P], F32, "ident")
-        make_identity(nc, ident[:])
         w4s_raw = held([P, N], U8, "w4s_raw")
         nc.gpsimd.memset(w4s_raw[:].bitcast(I32), 0)
         for q in range(QUADS):
-            nc.gpsimd.dma_start(out=w4s_raw[32 * q : 32 * q + 8, :].bitcast(I32),
-                                in_=w4_scales[:, 4 * q : 4 * q + 4, :].bitcast(I32))
+            nc.sync.dma_start(out=w4s_raw[32 * q : 32 * q + 8, :].bitcast(I32),
+                              in_=w4_scales[:, 4 * q : 4 * q + 4, :].bitcast(I32))
         gain_rows = held([P, P], F32, "gain_rows")
-        nc.vector.memset(gain_rows[:], 0.0)
-        nc.gpsimd.dma_start(out=gain_rows[0:PACK, :].rearrange("t (q i) -> t q i", i=8),
-                            in_=gain.rearrange("(q t i) -> t q i", t=PACK, i=8))
-        w2s_raw = held([P, PASSES * H // 4], I32, "w2s_raw")
-        nc.gpsimd.memset(w2s_raw[:], 0)
-        for q in range(QUADS):
-            nc.gpsimd.dma_start(out=w2s_raw[32 * q : 32 * q + 4, :].rearrange("r (a c) -> r a c", a=PASSES),
-                                in_=w2_scales[:, 4 * q : 4 * q + 4, :].bitcast(I32).rearrange("a r c -> r a c"))
+        nc.gpsimd.memset(gain_rows[:], 0.0)
+        nc.sync.dma_start(out=gain_rows[0:PACK, :].rearrange("t (q i) -> t q i", i=8),
+                          in_=gain.rearrange("(q t i) -> t q i", t=PACK, i=8))
+        nc.vector.memset(tab_sc[32:64, :].bitcast(I32), 0)
+        nc.vector.memset(tab_sc[64:P, :].bitcast(I32), 0)
+        ident = held([P, P], F32, "ident")
+        make_identity(nc, ident[:])
         v_s = [held([P, S], U8, "v_s%d" % a) for a in range(PASSES)]
         for a in range(PASSES):
-            nc.vector.memset(v_s[a][:].bitcast(I32), 0)
+            nc.gpsimd.memset(v_s[a][:].bitcast(I32), 0)
         gain_ps = psum.tile([P, P], F32, name="gain_ps")
         nc.tensor.transpose(gain_ps[:], gain_rows[:], ident[:])
 
@@ -95,26 +92,33 @@ def tile_list_boundary_marker_discrepancy_kernel(
                 nc.vector.tensor_copy(v_w[a][:, b * HALF : (b + 1) * HALF],
                                       tab_w[a][:].indirect(offs_sb[:, b * HALF // LANES : (b + 1) * HALF // LANES]))
 
-        nc.vector.tensor_copy(v_sc[:], tab_sc[:].indirect(offs_sb[:]))
-        for a in range(PASSES):
+        def move_scales(a):
             for q in range(QUADS):
                 row = 16 * a + 4 * q
-                nc.scalar.dma_start(out=v_s[a][32 * q : 32 * q + 4, :].bitcast(I32), in_=v_sc[row : row + 4, :].bitcast(I32))
-        w2_raw = shared([P, PASSES * H // 2], I32, "w2_raw", "third")
-        nc.sync.dma_start(out=w2_raw[:].rearrange("p (a c) -> p a c", a=PASSES),
-                          in_=w2_words.rearrange("a p c -> p a c").bitcast(I32))
-        gather_words(0)
-        w1_both = shared([P, PASSES, PACK, H], F32, "w1_both", "first")
-        w1_raw = [w1_both[:, a] for a in range(PASSES)]
-        for a in range(PASSES):
+                nc.sync.dma_start(out=v_s[a][32 * q : 32 * q + 4, :].bitcast(I32), in_=v_sc[row : row + 4, :].bitcast(I32))
+
+        def load_w1(a):
             nc.sync.dma_start(out=w1_raw[a], in_=w1[512 * a : 512 * (a + 1), :].rearrange("(p j) c -> p j c", j=PACK))
-        w4_q = held([P, PASSES * N], I32, "w4_q")
-        nc.vector.tensor_copy(w4_q[:].rearrange("p (a t m i) -> p a m t i", a=PASSES, t=PACK, i=4),
-                              w4_raw[:].rearrange("p (a m i t) -> p a m t i", a=PASSES, t=PACK, i=4))
-        w4_s = held([P, N], U8, "w4_s")
-        nc.vector.tensor_copy(w4_s[:].rearrange("p (t m) -> p t m", t=PACK), w4s_raw[:].rearrange("p (m t) -> p t m", t=PACK))
-        gather_words(1)
-        late = shared([P, 2, PACK, HALF], F32, "late", "second")
+
+        nc.vector.tensor_copy(v_sc[:], tab_sc[:].indirect(offs_sb[:]))
+        load_tab(1)
+        move_scales(0)
+        w2_both = staged([P, 3 * KB // 4], I32, "w2_both", 32 * KB)
+        w2_raw = w2_both[:, 0 : 2 * KB // 4]
+        w2s_raw = w2_both[:, 2 * KB // 4 : 3 * KB // 4]
+        nc.sync.dma_start(out=w2_raw.rearrange("p (a c) -> p a c", a=PASSES),
+                          in_=w2_words.rearrange("a p c -> p a c").bitcast(I32))
+        w1_both = staged([P, PASSES, PACK, H], F32, "w1_both", 35 * KB)
+        w1_raw = [w1_both[:, a] for a in range(PASSES)]
+        load_w1(0)
+        move_scales(1)
+        load_w1(1)
+        nc.gpsimd.memset(w2s_raw, 0)
+        for q in range(QUADS):
+            nc.sync.dma_start(out=w2s_raw[32 * q : 32 * q + 4, :].rearrange("r (a c) -> r a c", a=PASSES),
+                              in_=w2_scales[:, 4 * q : 4 * q + 4, :].bitcast(I32).rearrange("a r c -> r a c"))
+        gather_words(0)
+        late = staged([P, 2, PACK, HALF], F32, "late", 0)
         trust_sb = [late[:, 0]]
         w3_raw = late[:, 1]
         trust_rows = trust.rearrange("(p t) j -> p t j", t=PACK)
@@ -122,54 +126,78 @@ def tile_list_boundary_marker_discrepancy_kernel(
         w3_rows = w3.rearrange("(q s i) n -> s q i n", s=PACK, i=8)
         for s in range(PACK):
             nc.sync.dma_start(out=w3_raw[:, s, :], in_=w3_rows[s])
-        w2_q = held([P, PASSES * H * 2], U8, "w2_q")
+        w4_q = held([P, PASSES * N], I32, "w4_q")
+        nc.vector.tensor_copy(w4_q[:].rearrange("p (a t m i) -> p a m t i", a=PASSES, t=PACK, i=4),
+                              w4_raw[:].rearrange("p (a m i t) -> p a m t i", a=PASSES, t=PACK, i=4))
+        w4_s = held([P, N], U8, "w4_s")
+        nc.vector.tensor_copy(w4_s[:].rearrange("p (t m) -> p t m", t=PACK), w4s_raw[:].rearrange("p (m t) -> p t m", t=PACK))
+        gather_words(1)
+        trust_sb.append(staged([P, PACK, HALF], F32, "trust_late", 16 * KB)[:])
+        nc.sync.dma_start(out=trust_sb[1], in_=trust_rows[:, :, HALF:S])
+        w2_q = staged([P, PASSES * H * 2], U8, "w2_q", 24 * KB)
         nc.vector.tensor_copy(w2_q[:].bitcast(I32).rearrange("p (a t q i) -> p a t q i", a=PASSES, t=PACK, i=4),
-                              w2_raw[:].rearrange("p (a q t i) -> p a t q i", a=PASSES, t=PACK, i=4))
-        w2_s = held([P, PASSES * H], U8, "w2_s")
-        nc.vector.tensor_copy(w2_s[:].bitcast(I32).rearrange("p (a t q i) -> p a t q i", a=PASSES, t=PACK, i=2),
-                              w2s_raw[:].rearrange("p (a q t i) -> p a t q i", a=PASSES, t=PACK, i=2))
+                              w2_raw.rearrange("p (a q t i) -> p a t q i", a=PASSES, t=PACK, i=4))
 
         skip = [held([P, PACK, HALF], F32, "skip%d" % b) for b in range(2)]
-        for b in range(2):
+
+        def skip_product(b, ts):
             cols = slice(b * HALF, (b + 1) * HALF)
-            for t in range(PACK):
-                bank = psum.tile([P, HALF], F32, name="wide", bufs=2)
-                for a in range(PASSES):
-                    nc.tensor.matmul_mx(out=bank[:], lhsT=w4_q[:, a * N + t * P : a * N + (t + 1) * P].bitcast(FP8X4),
+            banks = {t: psum.tile([P, HALF], F32, name="bank", bufs=BANKS) for t in ts}
+            for a in range(PASSES):
+                for t in ts:
+                    nc.tensor.matmul_mx(out=banks[t][:], lhsT=w4_q[:, a * N + t * P : a * N + (t + 1) * P].bitcast(FP8X4),
                                         lhsT_scale=w4_s[4 * a : P, t * P : (t + 1) * P],
                                         rhs=v_w[a][:, cols].bitcast(FP8X4), rhs_scale=v_s[a][:, cols],
                                         start=(a == 0), stop=(a == PASSES - 1))
-                nc.scalar.activation(out=skip[b][:, t, :], in_=bank[:], func=ACT.Copy)
+            for t in ts:
+                nc.scalar.activation(out=skip[b][:, t, :], in_=banks[t][:], func=ACT.Copy)
+
+        skip_product(0, range(PACK))
+        skip_product(1, range(2))
 
         w1_q = {}
         w1_s = {}
+
+        def quantise_w1(a, u):
+            w1_q[a, u] = held([P, 2 * P], U32, "w1_q%d%d" % (a, u))
+            w1_s[a, u] = held([P, 2 * P], U8, "w1_s%d%d" % (a, u))
+            nc.vector.quantize_mx(out=w1_q[a, u][:].bitcast(FP8X4), scales=w1_s[a, u][:], in_=grouped[u][:])
+
         for a in range(PASSES):
             grouped = []
             for u in range(2):
-                g = held([P, 2 * P * PACK], BF16, "w1_g%d%d" % (a, u))
+                g = staged([P, 2 * P * PACK], BF16, "w1_g%d%d" % (a, u), (26, 51)[a] * KB + 2 * KB * u)
                 nc.vector.tensor_copy(
                     g[:].rearrange("p (e q i j) -> p e q j i", e=2, i=8, j=PACK),
                     w1_raw[a].rearrange("p j (q t i) -> p t q j i", t=PACK, i=8)[:, 2 * u : 2 * u + 2])
                 grouped.append(g)
-            for u in range(2):
-                w1_q[a, u] = held([P, 2 * P], U32, "w1_q%d%d" % (a, u))
-                w1_s[a, u] = held([P, 2 * P], U8, "w1_s%d%d" % (a, u))
-                nc.vector.quantize_mx(out=w1_q[a, u][:].bitcast(FP8X4), scales=w1_s[a, u][:], in_=grouped[u][:])
+                if a == 1:
+                    quantise_w1(a, u)
+            if a == 0:
+                quantise_w1(a, 0)
+                quantise_w1(a, 1)
+                w2_s = staged([P, PASSES * H], U8, "w2_s", 26 * KB)
+                nc.vector.tensor_copy(w2_s[:].bitcast(I32).rearrange("p (a t q i) -> p a t q i", a=PASSES, t=PACK, i=2),
+                                      w2s_raw.rearrange("p (a q t i) -> p a t q i", a=PASSES, t=PACK, i=2))
 
-        trust_sb.append(shared([P, PACK, HALF], F32, "trust_late", "first")[:])
-        nc.sync.dma_start(out=trust_sb[1], in_=trust_rows[:, :, HALF:S])
-
-        h_q = [held([P, HALF], U32, "h_q%d" % b) for b in range(2)]
-        h_s = [held([P, HALF], U8, "h_s%d" % b) for b in range(2)]
+        early_bf = held([P, (N + HALF) * PACK], BF16, "early_bf")
+        early_q = held([P, N + HALF], U32, "early_q")
+        early_s = held([P, N + HALF], U8, "early_s")
+        last_bf = held([P, HALF * PACK], BF16, "last_bf")
+        last_q = held([P, HALF], U32, "last_q")
+        last_s = held([P, HALF], U8, "last_s")
+        w3_g, w3_q, w3_s = early_bf[:, 0 : N * PACK], early_q[:, 0:N], early_s[:, 0:N]
+        h_bf = [early_bf[:, N * PACK : (N + HALF) * PACK], last_bf[:]]
+        h_q = [early_q[:, N : N + HALF], last_q[:]]
+        h_s = [early_s[:, N : N + HALF], last_s[:]]
         gain_tn = gain_ps[:, 0:PACK].unsqueeze(1).unsqueeze(3).to_broadcast([P, CHUNK // 2, PACK, 2])
         lesser = {}
-        h_bf = {}
 
         def products(c):
             cols = slice(c * CHUNK, (c + 1) * CHUNK)
             lesser[c] = ring.tile([P, PACK * CHUNK], F32, name="lesser")
             for u in range(2):
-                lin = psum.tile([P, 2, CHUNK], F32, name="lin", bufs=3)
+                lin = psum.tile([P, 2, CHUNK], F32, name="bank", bufs=BANKS)
                 for e in range(2):
                     t = 2 * u + e
                     for a in range(PASSES):
@@ -178,7 +206,7 @@ def tile_list_boundary_marker_discrepancy_kernel(
                                             lhsT_scale=w2_s[:, a * H + t * P : a * H + (t + 1) * P],
                                             rhs=v_w[a][:, cols].bitcast(FP8X4), rhs_scale=v_s[a][:, cols],
                                             start=(a == 0), stop=(a == PASSES - 1))
-                pre = psum.tile([P, 2, CHUNK], F32, name="pre", bufs=2)
+                pre = psum.tile([P, 2, CHUNK], F32, name="bank", bufs=BANKS)
                 for a in range(PASSES):
                     for e in range(2):
                         nc.tensor.matmul_mx(out=pre[:, e, :], lhsT=w1_q[a, u][:, e * P : (e + 1) * P].bitcast(FP8X4),
@@ -191,40 +219,34 @@ def tile_list_boundary_marker_discrepancy_kernel(
                                         lin[:].rearrange("p e n -> p (e n)"), bounded[:], ALU.min)
 
         def apply_gain(c):
-            h_bf[c] = ring.tile([P, CHUNK * PACK], BF16, name="h_bf", align_bytes=64)
-            nc.vector.tensor_tensor(h_bf[c][:].rearrange("p (c i t) -> p c t i", i=2, t=PACK),
+            dst = h_bf[c // 2][:, (c % 2) * CHUNK * PACK : (c % 2 + 1) * CHUNK * PACK]
+            nc.vector.tensor_tensor(dst.rearrange("p (c i t) -> p c t i", i=2, t=PACK),
                                     lesser[c][:].rearrange("p (t c i) -> p c t i", i=2, t=PACK), gain_tn, ALU.mult)
-
-        def quantise_h(c):
-            cols = slice((c % 2) * CHUNK, (c % 2 + 1) * CHUNK)
-            nc.vector.quantize_mx(out=h_q[c // 2][:, cols].bitcast(FP8X4), scales=h_s[c // 2][:, cols], in_=h_bf[c][:])
 
         def weigh_skip(b):
             for t in range(PACK):
-                nc.vector.tensor_tensor(skip[b][:, t, :], skip[b][:, t, :], trust_sb[b][:, t, :], ALU.mult)
-
-        w3_g = held([P, N * PACK], BF16, "w3_g")
-        w3_q = held([P, N], U32, "w3_q")
-        w3_s = held([P, N], U8, "w3_s")
+                for lo in range(0, HALF, CHUNK):
+                    part = skip[b][:, t, lo : lo + CHUNK]
+                    nc.gpsimd.tensor_tensor(part, part, trust_sb[b][:, t, lo : lo + CHUNK], ALU.mult)
 
         def round_w3(part):
             ms = slice(32 * part, 32 * (part + 1))
-            nc.scalar.activation(out=w3_g[:].rearrange("p (t m s) -> p m s t", t=PACK, s=PACK)[:, ms],
+            nc.scalar.activation(out=w3_g.rearrange("p (t m s) -> p m s t", t=PACK, s=PACK)[:, ms],
                                  in_=w3_raw.rearrange("p s (m t) -> p m s t", t=PACK)[:, ms], func=ACT.Copy)
 
+        weigh_skip(0)
         chunks = S // CHUNK
         for c in range(chunks):
             products(c)
-            if c > 0:
-                quantise_h(c - 1)
+            if c == chunks - 1:
+                nc.vector.quantize_mx(out=early_q[:].bitcast(FP8X4), scales=early_s[:], in_=early_bf[:])
             apply_gain(c)
-            if c >= 2:
-                round_w3(2 * (c - 2))
-                round_w3(2 * (c - 2) + 1)
-        weigh_skip(0)
-        quantise_h(chunks - 1)
-        nc.vector.quantize_mx(out=w3_q[:].bitcast(FP8X4), scales=w3_s[:], in_=w3_g[:])
-        weigh_skip(1)
+            if c == 0:
+                skip_product(1, range(2, PACK))
+                weigh_skip(1)
+            if c in (1, 2):
+                round_w3(2 * (c - 1))
+                round_w3(2 * (c - 1) + 1)
 
         g2 = [held([P, S], F32, "g2_%d" % t) for t in range(PACK)]
         y = held([P, PACK, M], F32, "y")
@@ -232,10 +254,10 @@ def tile_list_boundary_marker_discrepancy_kernel(
         first = {}
 
         def second_stage(t, b):
-            bank = psum.tile([P, HALF], F32, name="wide", bufs=2)
+            bank = psum.tile([P, HALF], F32, name="bank", bufs=BANKS)
             nc.tensor.matmul_mx(out=bank[:], lhsT=w3_q[:, t * P : (t + 1) * P].bitcast(FP8X4),
                                 lhsT_scale=w3_s[:, t * P : (t + 1) * P],
-                                rhs=h_q[b][:].bitcast(FP8X4), rhs_scale=h_s[b][:], start=True, stop=True)
+                                rhs=h_q[b].bitcast(FP8X4), rhs_scale=h_s[b], start=True, stop=True)
             nc.vector.tensor_tensor(g2[t][:, b * HALF : (b + 1) * HALF], bank[:], skip[b][:, t, :], ALU.subtract)
 
         def pick_first(t, lo, hi):
@@ -265,13 +287,14 @@ def tile_list_boundary_marker_discrepancy_kernel(
                     y[:, :, b * mid : (b + 1) * mid].rearrange("p t (c i) -> p c t i", i=2))
 
         second_stage(0, 0)
+        nc.vector.quantize_mx(out=last_q[:].bitcast(FP8X4), scales=last_s[:], in_=last_bf[:])
+        second_stage(1, 0)
         second_stage(0, 1)
         for t in range(2):
-            second_stage(t + 1, 0)
+            second_stage(t + 2, 0)
             pick_first(t, 0, M)
             second_stage(t + 1, 1)
             pick_second(t, 0, M)
-        second_stage(3, 0)
         pick_first(2, 0, mid)
         second_stage(3, 1)
         pick_second(2, 0, mid)

@@ -26,6 +26,7 @@ CHUNK = 256
 LANES = 16
 KB = 1024
 BANKS = 7
+ROWS = 32
 
 
 def tile_list_boundary_marker_discrepancy_kernel(
@@ -51,10 +52,12 @@ def tile_list_boundary_marker_discrepancy_kernel(
             return stage.tile(shape, dtype, name=name, align_bytes=64, offset=offset)
 
         nc.sync.dma_start(offs_sb[:], offs)
-        tab_sc = staged([P, T], U8, "tab_sc", 31 * KB + KB // 2)
-        nc.sync.dma_start(out=tab_sc[0:32, :].bitcast(I32), in_=tab_scales.rearrange("a q t -> (a q) t").bitcast(I32))
-        nc.sync.dma_start(pos1_sb[:], pos1)
-        nc.sync.dma_start(pos2_sb[:], pos2)
+        tab_sc = held([P, T], U8, "tab_sc")
+        nc.sync.dma_start(out=tab_sc[0:ROWS, :].bitcast(I32), in_=tab_scales.rearrange("a q t -> (a q) t").bitcast(I32))
+        w4s_raw = held([P, N], U8, "w4s_raw")
+        nc.sync.dma_start(out=w4s_raw[0:ROWS, :].bitcast(I32), in_=w4_scales.rearrange("a q c -> (a q) c").bitcast(I32))
+        w2s_raw = held([ROWS, H // 4], I32, "w2s_raw")
+        nc.sync.dma_start(out=w2s_raw[:], in_=w2_scales.rearrange("a q c -> (a q) c").bitcast(I32))
         tab_w = {}
 
         def load_tab(a):
@@ -62,30 +65,41 @@ def tile_list_boundary_marker_discrepancy_kernel(
             nc.sync.dma_start(out=tab_w[a][:].bitcast(I32), in_=tab_words[a].rearrange("p t i -> p (t i)").bitcast(I32))
 
         load_tab(0)
+        nc.sync.dma_start(pos1_sb[:], pos1)
+        nc.sync.dma_start(pos2_sb[:], pos2)
+        w2_raw = held([P, PASSES * H // 2], I32, "w2_raw")
+        nc.sync.dma_start(out=w2_raw[:].rearrange("p (a c) -> p a c", a=PASSES),
+                          in_=w2_words.rearrange("a p c -> p a c").bitcast(I32))
         w4_raw = held([P, PASSES * N], I32, "w4_raw")
         nc.sync.dma_start(out=w4_raw[:].rearrange("p (a c) -> p a c", a=PASSES),
                           in_=w4_words.rearrange("a p c i -> p a (c i)").bitcast(I32))
-        w4s_raw = held([P, N], U8, "w4s_raw")
-        nc.gpsimd.memset(w4s_raw[:].bitcast(I32), 0)
-        for q in range(QUADS):
-            nc.sync.dma_start(out=w4s_raw[32 * q : 32 * q + 8, :].bitcast(I32),
-                              in_=w4_scales[:, 4 * q : 4 * q + 4, :].bitcast(I32))
         gain_rows = held([P, P], F32, "gain_rows")
         nc.gpsimd.memset(gain_rows[:], 0.0)
-        nc.sync.dma_start(out=gain_rows[0:PACK, :].rearrange("t (q i) -> t q i", i=8),
-                          in_=gain.rearrange("(q t i) -> t q i", t=PACK, i=8))
-        nc.vector.memset(tab_sc[32:64, :].bitcast(I32), 0)
-        nc.vector.memset(tab_sc[64:P, :].bitcast(I32), 0)
+        nc.gpsimd.dma_start(out=gain_rows[0:PACK, :].rearrange("t (q i) -> t q i", i=8),
+                            in_=gain.rearrange("(q t i) -> t q i", t=PACK, i=8))
+        for tile in (tab_sc, w4s_raw):
+            nc.vector.memset(tile[ROWS:64, :].bitcast(I32), 0)
+            nc.vector.memset(tile[64:P, :].bitcast(I32), 0)
         ident = held([P, P], F32, "ident")
         make_identity(nc, ident[:])
-        v_s = [held([P, S], U8, "v_s%d" % a) for a in range(PASSES)]
+        scale = [held([P, S + N + H], U8, "scale%d" % a) for a in range(PASSES)]
         for a in range(PASSES):
-            nc.gpsimd.memset(v_s[a][:].bitcast(I32), 0)
+            nc.gpsimd.memset(scale[a][:].bitcast(I32), 0)
+        v_s = [scale[a][:, 0:S] for a in range(PASSES)]
+        w4_s = [scale[a][:, S : S + N] for a in range(PASSES)]
+        w2_s = [scale[a][:, S + N : S + N + H] for a in range(PASSES)]
         gain_ps = psum.tile([P, P], F32, name="gain_ps")
         nc.tensor.transpose(gain_ps[:], gain_rows[:], ident[:])
 
+        rows = held([P, S + N + H], U8, "rows")
+        nc.vector.tensor_copy(rows[:, S : S + N].rearrange("p (t m) -> p t m", t=PACK),
+                              w4s_raw[:].rearrange("p (m t) -> p t m", t=PACK))
+        nc.vector.tensor_copy(rows[0:ROWS, S + N : S + N + H].bitcast(I32).rearrange("p (t q i) -> p t q i", t=PACK, i=2),
+                              w2s_raw[:].rearrange("p (q t i) -> p t q i", t=PACK, i=2))
         v_w = [held([P, S], U32, "v_w%d" % a) for a in range(PASSES)]
-        v_sc = held([P, S], U8, "v_sc")
+        v_sc = staged([P, S], U8, "v_sc", 32 * KB - S // 2)
+        nc.vector.tensor_copy(v_sc[:], tab_sc[:].indirect(offs_sb[:]))
+        nc.vector.tensor_copy(rows[0:ROWS, 0:S].bitcast(I32), v_sc[0:ROWS, :].bitcast(I32))
 
         def gather_words(a):
             for b in range(2):
@@ -95,28 +109,15 @@ def tile_list_boundary_marker_discrepancy_kernel(
         def move_scales(a):
             for q in range(QUADS):
                 row = 16 * a + 4 * q
-                nc.sync.dma_start(out=v_s[a][32 * q : 32 * q + 4, :].bitcast(I32), in_=v_sc[row : row + 4, :].bitcast(I32))
+                nc.sync.dma_start(out=scale[a][32 * q : 32 * q + 4, :].bitcast(I32), in_=rows[row : row + 4, :].bitcast(I32))
 
-        def load_w1(a):
-            nc.sync.dma_start(out=w1_raw[a], in_=w1[512 * a : 512 * (a + 1), :].rearrange("(p j) c -> p j c", j=PACK))
-
-        nc.vector.tensor_copy(v_sc[:], tab_sc[:].indirect(offs_sb[:]))
-        load_tab(1)
         move_scales(0)
-        w2_both = staged([P, 3 * KB // 4], I32, "w2_both", 32 * KB)
-        w2_raw = w2_both[:, 0 : 2 * KB // 4]
-        w2s_raw = w2_both[:, 2 * KB // 4 : 3 * KB // 4]
-        nc.sync.dma_start(out=w2_raw.rearrange("p (a c) -> p a c", a=PASSES),
-                          in_=w2_words.rearrange("a p c -> p a c").bitcast(I32))
-        w1_both = staged([P, PASSES, PACK, H], F32, "w1_both", 35 * KB)
-        w1_raw = [w1_both[:, a] for a in range(PASSES)]
-        load_w1(0)
+        load_tab(1)
         move_scales(1)
-        load_w1(1)
-        nc.gpsimd.memset(w2s_raw, 0)
-        for q in range(QUADS):
-            nc.sync.dma_start(out=w2s_raw[32 * q : 32 * q + 4, :].rearrange("r (a c) -> r a c", a=PASSES),
-                              in_=w2_scales[:, 4 * q : 4 * q + 4, :].bitcast(I32).rearrange("a r c -> r a c"))
+        w1_both = staged([P, PASSES, PACK, H], F32, "w1_both", 32 * KB)
+        w1_raw = [w1_both[:, a] for a in range(PASSES)]
+        for a in range(PASSES):
+            nc.sync.dma_start(out=w1_raw[a], in_=w1[512 * a : 512 * (a + 1), :].rearrange("(p j) c -> p j c", j=PACK))
         gather_words(0)
         late = staged([P, 2, PACK, HALF], F32, "late", 0)
         trust_sb = [late[:, 0]]
@@ -129,14 +130,12 @@ def tile_list_boundary_marker_discrepancy_kernel(
         w4_q = held([P, PASSES * N], I32, "w4_q")
         nc.vector.tensor_copy(w4_q[:].rearrange("p (a t m i) -> p a m t i", a=PASSES, t=PACK, i=4),
                               w4_raw[:].rearrange("p (a m i t) -> p a m t i", a=PASSES, t=PACK, i=4))
-        w4_s = held([P, N], U8, "w4_s")
-        nc.vector.tensor_copy(w4_s[:].rearrange("p (t m) -> p t m", t=PACK), w4s_raw[:].rearrange("p (m t) -> p t m", t=PACK))
+        w2_q = held([P, PASSES * H * 2], U8, "w2_q")
+        nc.vector.tensor_copy(w2_q[:].bitcast(I32).rearrange("p (a t q i) -> p a t q i", a=PASSES, t=PACK, i=4),
+                              w2_raw[:].rearrange("p (a q t i) -> p a t q i", a=PASSES, t=PACK, i=4))
         gather_words(1)
         trust_sb.append(staged([P, PACK, HALF], F32, "trust_late", 16 * KB)[:])
         nc.sync.dma_start(out=trust_sb[1], in_=trust_rows[:, :, HALF:S])
-        w2_q = staged([P, PASSES * H * 2], U8, "w2_q", 24 * KB)
-        nc.vector.tensor_copy(w2_q[:].bitcast(I32).rearrange("p (a t q i) -> p a t q i", a=PASSES, t=PACK, i=4),
-                              w2_raw.rearrange("p (a q t i) -> p a t q i", a=PASSES, t=PACK, i=4))
 
         skip = [held([P, PACK, HALF], F32, "skip%d" % b) for b in range(2)]
 
@@ -146,7 +145,7 @@ def tile_list_boundary_marker_discrepancy_kernel(
             for a in range(PASSES):
                 for t in ts:
                     nc.tensor.matmul_mx(out=banks[t][:], lhsT=w4_q[:, a * N + t * P : a * N + (t + 1) * P].bitcast(FP8X4),
-                                        lhsT_scale=w4_s[4 * a : P, t * P : (t + 1) * P],
+                                        lhsT_scale=w4_s[a][:, t * P : (t + 1) * P],
                                         rhs=v_w[a][:, cols].bitcast(FP8X4), rhs_scale=v_s[a][:, cols],
                                         start=(a == 0), stop=(a == PASSES - 1))
             for t in ts:
@@ -154,6 +153,7 @@ def tile_list_boundary_marker_discrepancy_kernel(
 
         skip_product(0, range(PACK))
         skip_product(1, range(2))
+        skip_product(1, range(2, PACK))
 
         w1_q = {}
         w1_s = {}
@@ -166,19 +166,17 @@ def tile_list_boundary_marker_discrepancy_kernel(
         for a in range(PASSES):
             grouped = []
             for u in range(2):
-                g = staged([P, 2 * P * PACK], BF16, "w1_g%d%d" % (a, u), (26, 51)[a] * KB + 2 * KB * u)
-                nc.vector.tensor_copy(
-                    g[:].rearrange("p (e q i j) -> p e q j i", e=2, i=8, j=PACK),
-                    w1_raw[a].rearrange("p j (q t i) -> p t q j i", t=PACK, i=8)[:, 2 * u : 2 * u + 2])
+                g = staged([P, 2 * P * PACK], BF16, "w1_g%d%d" % (a, u), (26, 48)[a] * KB + 2 * KB * u)
+                for e in range(2):
+                    nc.vector.tensor_copy(
+                        g[:].rearrange("p (e q z i j) -> p e q z j i", e=2, z=2, i=4, j=PACK)[:, e],
+                        w1_raw[a].rearrange("p j (q t z i) -> p t q z j i", t=PACK, z=2, i=4)[:, 2 * u + e])
                 grouped.append(g)
                 if a == 1:
                     quantise_w1(a, u)
             if a == 0:
                 quantise_w1(a, 0)
                 quantise_w1(a, 1)
-                w2_s = staged([P, PASSES * H], U8, "w2_s", 26 * KB)
-                nc.vector.tensor_copy(w2_s[:].bitcast(I32).rearrange("p (a t q i) -> p a t q i", a=PASSES, t=PACK, i=2),
-                                      w2s_raw.rearrange("p (a q t i) -> p a t q i", a=PASSES, t=PACK, i=2))
 
         early_bf = held([P, (N + HALF) * PACK], BF16, "early_bf")
         early_q = held([P, N + HALF], U32, "early_q")
@@ -190,22 +188,13 @@ def tile_list_boundary_marker_discrepancy_kernel(
         h_bf = [early_bf[:, N * PACK : (N + HALF) * PACK], last_bf[:]]
         h_q = [early_q[:, N : N + HALF], last_q[:]]
         h_s = [early_s[:, N : N + HALF], last_s[:]]
-        gain_tn = gain_ps[:, 0:PACK].unsqueeze(1).unsqueeze(3).to_broadcast([P, CHUNK // 2, PACK, 2])
+        gain_tn = gain_ps[:, 0:PACK].rearrange("p (u e) -> p u e", u=2).unsqueeze(1).to_broadcast([P, CHUNK, 2, 2])
         lesser = {}
 
         def products(c):
             cols = slice(c * CHUNK, (c + 1) * CHUNK)
-            lesser[c] = ring.tile([P, PACK * CHUNK], F32, name="lesser")
+            lesser[c] = ring.tile([P, 2, CHUNK, 2], F32, name="lesser")
             for u in range(2):
-                lin = psum.tile([P, 2, CHUNK], F32, name="bank", bufs=BANKS)
-                for e in range(2):
-                    t = 2 * u + e
-                    for a in range(PASSES):
-                        nc.tensor.matmul_mx(out=lin[:, e, :],
-                                            lhsT=w2_q[:, 2 * (a * H + t * P) : 2 * (a * H + (t + 1) * P)].bitcast(FP4X4),
-                                            lhsT_scale=w2_s[:, a * H + t * P : a * H + (t + 1) * P],
-                                            rhs=v_w[a][:, cols].bitcast(FP8X4), rhs_scale=v_s[a][:, cols],
-                                            start=(a == 0), stop=(a == PASSES - 1))
                 pre = psum.tile([P, 2, CHUNK], F32, name="bank", bufs=BANKS)
                 for a in range(PASSES):
                     for e in range(2):
@@ -213,15 +202,23 @@ def tile_list_boundary_marker_discrepancy_kernel(
                                             lhsT_scale=w1_s[a, u][:, e * P : (e + 1) * P],
                                             rhs=v_w[a][:, cols].bitcast(FP8X4), rhs_scale=v_s[a][:, cols],
                                             start=(a == 0 and e == 0), stop=(a == PASSES - 1 and e == 1))
-                bounded = ring.tile([P, 2 * CHUNK], F32, name="bounded", bufs=3)
-                nc.scalar.activation(out=bounded[:], in_=pre[:].rearrange("p e n -> p (e n)"), func=ACT.Tanh)
-                nc.vector.tensor_tensor(lesser[c][:, 2 * u * CHUNK : 2 * (u + 1) * CHUNK],
-                                        lin[:].rearrange("p e n -> p (e n)"), bounded[:], ALU.min)
+                lin = psum.tile([P, 2, CHUNK], F32, name="bank", bufs=BANKS)
+                for e in range(2):
+                    t = 2 * u + e
+                    for a in range(PASSES):
+                        nc.tensor.matmul_mx(out=lin[:, e, :],
+                                            lhsT=w2_q[:, 2 * (a * H + t * P) : 2 * (a * H + (t + 1) * P)].bitcast(FP4X4),
+                                            lhsT_scale=w2_s[a][:, t * P : (t + 1) * P],
+                                            rhs=v_w[a][:, cols].bitcast(FP8X4), rhs_scale=v_s[a][:, cols],
+                                            start=(a == 0), stop=(a == PASSES - 1))
+                bounded = ring.tile([P, CHUNK, 2], F32, name="bounded", bufs=3)
+                nc.scalar.activation(out=bounded[:], in_=pre[:].rearrange("p e n -> p n e"), func=ACT.Tanh)
+                nc.vector.tensor_tensor(lesser[c][:, u], lin[:].rearrange("p e n -> p n e"), bounded[:], ALU.min)
 
         def apply_gain(c):
             dst = h_bf[c // 2][:, (c % 2) * CHUNK * PACK : (c % 2 + 1) * CHUNK * PACK]
-            nc.vector.tensor_tensor(dst.rearrange("p (c i t) -> p c t i", i=2, t=PACK),
-                                    lesser[c][:].rearrange("p (t c i) -> p c t i", i=2, t=PACK), gain_tn, ALU.mult)
+            nc.vector.tensor_tensor(dst.rearrange("p (n u e) -> p n u e", u=2, e=2),
+                                    lesser[c][:].rearrange("p u n e -> p n u e"), gain_tn, ALU.mult)
 
         def weigh_skip(b):
             for t in range(PACK):
@@ -231,19 +228,17 @@ def tile_list_boundary_marker_discrepancy_kernel(
 
         def round_w3(part):
             ms = slice(32 * part, 32 * (part + 1))
-            nc.scalar.activation(out=w3_g.rearrange("p (t m s) -> p m s t", t=PACK, s=PACK)[:, ms],
-                                 in_=w3_raw.rearrange("p s (m t) -> p m s t", t=PACK)[:, ms], func=ACT.Copy)
+            nc.scalar.activation(out=w3_g.rearrange("p (t m s) -> p m t s", t=PACK, s=PACK)[:, ms],
+                                 in_=w3_raw.rearrange("p s (m t) -> p m t s", t=PACK)[:, ms], func=ACT.Copy)
 
         weigh_skip(0)
+        weigh_skip(1)
         chunks = S // CHUNK
         for c in range(chunks):
             products(c)
             if c == chunks - 1:
                 nc.vector.quantize_mx(out=early_q[:].bitcast(FP8X4), scales=early_s[:], in_=early_bf[:])
             apply_gain(c)
-            if c == 0:
-                skip_product(1, range(2, PACK))
-                weigh_skip(1)
             if c in (1, 2):
                 round_w3(2 * (c - 1))
                 round_w3(2 * (c - 1) + 1)
@@ -283,8 +278,8 @@ def tile_list_boundary_marker_discrepancy_kernel(
             nc.sync.dma_start(out=words_out[:, cols], in_=y_q[:, cols].bitcast(I32))
 
         def y_views(b):
-            return (y_bf[b][:].rearrange("p (c i t) -> p c t i", i=2, t=PACK),
-                    y[:, :, b * mid : (b + 1) * mid].rearrange("p t (c i) -> p c t i", i=2))
+            return (y_bf[b][:].rearrange("p (c i t) -> p c t i", i=4, t=PACK),
+                    y[:, :, b * mid : (b + 1) * mid].rearrange("p t (c i) -> p c t i", i=4))
 
         second_stage(0, 0)
         nc.vector.quantize_mx(out=last_q[:].bitcast(FP8X4), scales=last_s[:], in_=last_bf[:])

@@ -96,14 +96,14 @@ def tile_list_boundary_marker_discrepancy_kernel(
                               w4s_raw[:].rearrange("p (m t) -> p t m", t=PACK))
         nc.vector.tensor_copy(rows[0:ROWS, S + N : S + N + H].bitcast(I32).rearrange("p (t q i) -> p t q i", t=PACK, i=2),
                               w2s_raw[:].rearrange("p (q t i) -> p t q i", t=PACK, i=2))
-        v_w = [held([P, S], U32, "v_w%d" % a) for a in range(PASSES)]
+        v_w = [[held([P, HALF], U32, "v_w%d%d" % (a, b)) for b in range(2)] for a in range(PASSES)]
         v_sc = staged([P, S], U8, "v_sc", 32 * KB - S // 2)
         nc.vector.tensor_copy(v_sc[:], tab_sc[:].indirect(offs_sb[:]))
         nc.vector.tensor_copy(rows[0:ROWS, 0:S].bitcast(I32), v_sc[0:ROWS, :].bitcast(I32))
 
         def gather_words(a):
             for b in range(2):
-                nc.vector.tensor_copy(v_w[a][:, b * HALF : (b + 1) * HALF],
+                nc.vector.tensor_copy(v_w[a][b][:],
                                       tab_w[a][:].indirect(offs_sb[:, b * HALF // LANES : (b + 1) * HALF // LANES]))
 
         def move_scales(a):
@@ -119,11 +119,10 @@ def tile_list_boundary_marker_discrepancy_kernel(
         for a in range(PASSES):
             nc.sync.dma_start(out=w1_raw[a], in_=w1[512 * a : 512 * (a + 1), :].rearrange("(p j) c -> p j c", j=PACK))
         gather_words(0)
-        late = staged([P, 2, PACK, HALF], F32, "late", 0)
-        trust_sb = [late[:, 0]]
-        w3_raw = late[:, 1]
+        trust_sb = [staged([P, 2, S], F32, "trust_sb0", 0)]
+        w3_raw = staged([P, PACK, N], F32, "w3_raw", 8 * KB)
         trust_rows = trust.rearrange("(p t) j -> p t j", t=PACK)
-        nc.sync.dma_start(out=trust_sb[0], in_=trust_rows[:, :, 0:HALF])
+        nc.sync.dma_start(out=trust_sb[0][:], in_=trust_rows[:, 0:2, :])
         w3_rows = w3.rearrange("(q s i) n -> s q i n", s=PACK, i=8)
         for s in range(PACK):
             nc.sync.dma_start(out=w3_raw[:, s, :], in_=w3_rows[s])
@@ -134,10 +133,10 @@ def tile_list_boundary_marker_discrepancy_kernel(
         nc.vector.tensor_copy(w2_q[:].bitcast(I32).rearrange("p (a t q i) -> p a t q i", a=PASSES, t=PACK, i=4),
                               w2_raw[:].rearrange("p (a q t i) -> p a t q i", a=PASSES, t=PACK, i=4))
         gather_words(1)
-        trust_sb.append(staged([P, PACK, HALF], F32, "trust_late", 16 * KB)[:])
-        nc.sync.dma_start(out=trust_sb[1], in_=trust_rows[:, :, HALF:S])
+        trust_sb.append(staged([P, 2, S], F32, "trust_sb1", 16 * KB))
+        nc.sync.dma_start(out=trust_sb[1][:], in_=trust_rows[:, 2:PACK, :])
 
-        skip = [held([P, PACK, HALF], F32, "skip%d" % b) for b in range(2)]
+        skip = [held([P, S], F32, "skip%d" % t) for t in range(PACK)]
 
         def skip_product(b, ts):
             cols = slice(b * HALF, (b + 1) * HALF)
@@ -146,10 +145,10 @@ def tile_list_boundary_marker_discrepancy_kernel(
                 for t in ts:
                     nc.tensor.matmul_mx(out=banks[t][:], lhsT=w4_q[:, a * N + t * P : a * N + (t + 1) * P].bitcast(FP8X4),
                                         lhsT_scale=w4_s[a][:, t * P : (t + 1) * P],
-                                        rhs=v_w[a][:, cols].bitcast(FP8X4), rhs_scale=v_s[a][:, cols],
+                                        rhs=v_w[a][b][:].bitcast(FP8X4), rhs_scale=v_s[a][:, cols],
                                         start=(a == 0), stop=(a == PASSES - 1))
             for t in ts:
-                nc.scalar.activation(out=skip[b][:, t, :], in_=banks[t][:], func=ACT.Copy)
+                nc.scalar.activation(out=skip[t][:, cols], in_=banks[t][:], func=ACT.Copy)
 
         skip_product(0, range(PACK))
         skip_product(1, range(2))
@@ -178,29 +177,25 @@ def tile_list_boundary_marker_discrepancy_kernel(
                 quantise_w1(a, 0)
                 quantise_w1(a, 1)
 
-        early_bf = held([P, (N + HALF) * PACK], BF16, "early_bf")
-        early_q = held([P, N + HALF], U32, "early_q")
-        early_s = held([P, N + HALF], U8, "early_s")
-        last_bf = held([P, HALF * PACK], BF16, "last_bf")
-        last_q = held([P, HALF], U32, "last_q")
-        last_s = held([P, HALF], U8, "last_s")
-        w3_g, w3_q, w3_s = early_bf[:, 0 : N * PACK], early_q[:, 0:N], early_s[:, 0:N]
-        h_bf = [early_bf[:, N * PACK : (N + HALF) * PACK], last_bf[:]]
-        h_q = [early_q[:, N : N + HALF], last_q[:]]
-        h_s = [early_s[:, N : N + HALF], last_s[:]]
+        h_bf = [held([P, HALF * PACK], BF16, "h_bf%d" % b) for b in range(2)]
+        h_q = [held([P, HALF], U32, "h_q%d" % b) for b in range(2)]
+        h_s = [held([P, HALF], U8, "h_s%d" % b) for b in range(2)]
+        w3_q = held([P, N], U32, "w3_q")
+        w3_s = held([P, N], U8, "w3_s")
         gain_tn = gain_ps[:, 0:PACK].rearrange("p (u e) -> p u e", u=2).unsqueeze(1).to_broadcast([P, CHUNK, 2, 2])
         lesser = {}
 
         def products(c):
             cols = slice(c * CHUNK, (c + 1) * CHUNK)
-            lesser[c] = ring.tile([P, 2, CHUNK, 2], F32, name="lesser")
+            moving = [v_w[a][c // 2][:, (c % 2) * CHUNK : (c % 2 + 1) * CHUNK].bitcast(FP8X4) for a in range(PASSES)]
+            lesser[c] = ring.tile([P, 2, CHUNK, 2], F32, name="lesser", align_bytes=64)
             for u in range(2):
                 pre = psum.tile([P, 2, CHUNK], F32, name="bank", bufs=BANKS)
                 for a in range(PASSES):
                     for e in range(2):
                         nc.tensor.matmul_mx(out=pre[:, e, :], lhsT=w1_q[a, u][:, e * P : (e + 1) * P].bitcast(FP8X4),
                                             lhsT_scale=w1_s[a, u][:, e * P : (e + 1) * P],
-                                            rhs=v_w[a][:, cols].bitcast(FP8X4), rhs_scale=v_s[a][:, cols],
+                                            rhs=moving[a], rhs_scale=v_s[a][:, cols],
                                             start=(a == 0 and e == 0), stop=(a == PASSES - 1 and e == 1))
                 lin = psum.tile([P, 2, CHUNK], F32, name="bank", bufs=BANKS)
                 for e in range(2):
@@ -209,7 +204,7 @@ def tile_list_boundary_marker_discrepancy_kernel(
                         nc.tensor.matmul_mx(out=lin[:, e, :],
                                             lhsT=w2_q[:, 2 * (a * H + t * P) : 2 * (a * H + (t + 1) * P)].bitcast(FP4X4),
                                             lhsT_scale=w2_s[a][:, t * P : (t + 1) * P],
-                                            rhs=v_w[a][:, cols].bitcast(FP8X4), rhs_scale=v_s[a][:, cols],
+                                            rhs=moving[a], rhs_scale=v_s[a][:, cols],
                                             start=(a == 0), stop=(a == PASSES - 1))
                 bounded = ring.tile([P, CHUNK, 2], F32, name="bounded", bufs=3)
                 nc.scalar.activation(out=bounded[:], in_=pre[:].rearrange("p e n -> p n e"), func=ACT.Tanh)
@@ -220,28 +215,30 @@ def tile_list_boundary_marker_discrepancy_kernel(
             nc.vector.tensor_tensor(dst.rearrange("p (n u e) -> p n u e", u=2, e=2),
                                     lesser[c][:].rearrange("p u n e -> p n u e"), gain_tn, ALU.mult)
 
-        def weigh_skip(b):
-            for t in range(PACK):
-                for lo in range(0, HALF, CHUNK):
-                    part = skip[b][:, t, lo : lo + CHUNK]
-                    nc.gpsimd.tensor_tensor(part, part, trust_sb[b][:, t, lo : lo + CHUNK], ALU.mult)
+        def quantise_h(b):
+            nc.vector.quantize_mx(out=h_q[b][:].bitcast(FP8X4), scales=h_s[b][:], in_=h_bf[b][:])
 
         def round_w3(part):
             ms = slice(32 * part, 32 * (part + 1))
-            nc.scalar.activation(out=w3_g.rearrange("p (t m s) -> p m t s", t=PACK, s=PACK)[:, ms],
-                                 in_=w3_raw.rearrange("p s (m t) -> p m t s", t=PACK)[:, ms], func=ACT.Copy)
+            nc.scalar.activation(out=w3_g[:].rearrange("p (t m s) -> p m t s", t=PACK, s=PACK)[:, ms],
+                                 in_=w3_raw[:].rearrange("p s (m t) -> p m t s", t=PACK)[:, ms], func=ACT.Copy)
 
-        weigh_skip(0)
-        weigh_skip(1)
+        for t in range(PACK):
+            for b in range(2):
+                cols = slice(b * HALF, (b + 1) * HALF)
+                nc.gpsimd.tensor_tensor(skip[t][:, cols], skip[t][:, cols], trust_sb[t // 2][:, t % 2, cols], ALU.mult)
         chunks = S // CHUNK
         for c in range(chunks):
             products(c)
-            if c == chunks - 1:
-                nc.vector.quantize_mx(out=early_q[:].bitcast(FP8X4), scales=early_s[:], in_=early_bf[:])
+            if c == 2:
+                quantise_h(0)
+                w3_g = ring.tile([P, N * PACK], BF16, name="w3_g", tag="lesser", align_bytes=64)
             apply_gain(c)
-            if c in (1, 2):
-                round_w3(2 * (c - 1))
-                round_w3(2 * (c - 1) + 1)
+            if c >= 2:
+                round_w3(2 * (c - 2))
+                round_w3(2 * (c - 2) + 1)
+        nc.vector.quantize_mx(out=w3_q[:].bitcast(FP8X4), scales=w3_s[:], in_=w3_g[:])
+        quantise_h(1)
 
         g2 = [held([P, S], F32, "g2_%d" % t) for t in range(PACK)]
         y = held([P, PACK, M], F32, "y")
@@ -252,8 +249,8 @@ def tile_list_boundary_marker_discrepancy_kernel(
             bank = psum.tile([P, HALF], F32, name="bank", bufs=BANKS)
             nc.tensor.matmul_mx(out=bank[:], lhsT=w3_q[:, t * P : (t + 1) * P].bitcast(FP8X4),
                                 lhsT_scale=w3_s[:, t * P : (t + 1) * P],
-                                rhs=h_q[b].bitcast(FP8X4), rhs_scale=h_s[b], start=True, stop=True)
-            nc.vector.tensor_tensor(g2[t][:, b * HALF : (b + 1) * HALF], bank[:], skip[b][:, t, :], ALU.subtract)
+                                rhs=h_q[b][:].bitcast(FP8X4), rhs_scale=h_s[b][:], start=True, stop=True)
+            nc.vector.tensor_tensor(g2[t][:, b * HALF : (b + 1) * HALF], bank[:], skip[t][:, b * HALF : (b + 1) * HALF], ALU.subtract)
 
         def pick_first(t, lo, hi):
             first[t, lo] = ring.tile([P, M], F32, name="first", bufs=3)
@@ -282,7 +279,6 @@ def tile_list_boundary_marker_discrepancy_kernel(
                     y[:, :, b * mid : (b + 1) * mid].rearrange("p t (c i) -> p c t i", i=4))
 
         second_stage(0, 0)
-        nc.vector.quantize_mx(out=last_q[:].bitcast(FP8X4), scales=last_s[:], in_=last_bf[:])
         second_stage(1, 0)
         second_stage(0, 1)
         for t in range(2):

from contextlib import ExitStack

import concourse.mybir as mybir
from concourse.masks import make_identity

K, H, N, T, S, M = 1024, 512, 512, 4096, 1024, 512
FLOPS = 2 * S * (K * H + K * H + K * N + H * N)

F32 = mybir.dt.float32
BF16 = mybir.dt.bfloat16
I32 = mybir.dt.int32
U32 = mybir.dt.uint32
U16 = mybir.dt.uint16
U8 = mybir.dt.uint8
FP8X4 = mybir.dt.float8_e4m3fn_x4
FP4X4 = mybir.dt.float4_e2m1fn_x4
ALU = mybir.AluOpType
ACT = mybir.ActivationFunctionType

P = 128
PACK = 4
PASSES = K // (P * PACK)
QUADS = 4
HALF = 512
CHUNK = 256
LANES = 16
KB = 1024
BANKS = 7
ROWS = 32


def tile_list_boundary_marker_discrepancy_kernel(
    tc, tab_words, tab_scales, offs, pos1, pos2, w1, w2_words, w2_scales, gain, w3, w4_words, w4_scales, trust,
    out_0, out_1, out_2,
):
    nc = tc.nc
    with ExitStack() as ctx:
        lists = ctx.enter_context(tc.tile_pool(name="lists", bufs=1))
        keep = ctx.enter_context(tc.tile_pool(name="keep", bufs=1))
        stage = ctx.enter_context(tc.tile_pool(name="stage", bufs=1))
        ring = ctx.enter_context(tc.tile_pool(name="ring", bufs=2))
        psum = ctx.enter_context(tc.psum_pool(name="psum", bufs=1))

        def held(shape, dtype, name):
            return keep.tile(shape, dtype, name=name, align_bytes=64)

        offs_sb = lists.tile([P, S // LANES], U16, name="offs_sb")
        pos1_sb = lists.tile([P, M // LANES], U16, name="pos1_sb")
        pos2_sb = lists.tile([P, M // LANES], U16, name="pos2_sb")

        def staged(shape, dtype, name, offset):
            return stage.tile(shape, dtype, name=name, align_bytes=64, offset=offset)

        nc.sync.dma_start(offs_sb[:], offs)
        tab_sc = held([P, T], U8, "tab_sc")
        nc.sync.dma_start(out=tab_sc[0:ROWS, :].bitcast(I32), in_=tab_scales.rearrange("a q t -> (a q) t").bitcast(I32))
        w4s_raw = held([P, N], U8, "w4s_raw")
        nc.sync.dma_start(out=w4s_raw[0:ROWS, :].bitcast(I32), in_=w4_scales.rearrange("a q c -> (a q) c").bitcast(I32))
        w2s_raw = held([ROWS, H // 4], I32, "w2s_raw")
        nc.sync.dma_start(out=w2s_raw[:], in_=w2_scales.rearrange("a q c -> (a q) c").bitcast(I32))
        tab_w = {}

        def load_tab(a):
            tab_w[a] = staged([P, T], U32, "tab_w%d" % a, 16 * KB * a)
            nc.sync.dma_start(out=tab_w[a][:].bitcast(I32), in_=tab_words[a].rearrange("p t i -> p (t i)").bitcast(I32))

        load_tab(0)
        nc.sync.dma_start(pos1_sb[:], pos1)
        nc.sync.dma_start(pos2_sb[:], pos2)
        w2_raw = held([P, PASSES * H // 2], I32, "w2_raw")
        nc.sync.dma_start(out=w2_raw[:].rearrange("p (a c) -> p a c", a=PASSES),
                          in_=w2_words.rearrange("a p c -> p a c").bitcast(I32))
        w4_raw = held([P, PASSES * N], I32, "w4_raw")
        nc.sync.dma_start(out=w4_raw[:].rearrange("p (a c) -> p a c", a=PASSES),
                          in_=w4_words.rearrange("a p c i -> p a (c i)").bitcast(I32))
        gain_rows = held([P, P], F32, "gain_rows")
        nc.gpsimd.memset(gain_rows[:], 0.0)
        nc.gpsimd.dma_start(out=gain_rows[0:PACK, :].rearrange("t (q i) -> t q i", i=8),
                            in_=gain.rearrange("(q t i) -> t q i", t=PACK, i=8))
        for tile in (tab_sc, w4s_raw):
            nc.vector.memset(tile[ROWS:64, :].bitcast(I32), 0)
            nc.vector.memset(tile[64:P, :].bitcast(I32), 0)
        ident = held([P, P], F32, "ident")
        make_identity(nc, ident[:])
        scale = [held([P, S + N + H], U8, "scale%d" % a) for a in range(PASSES)]
        for a in range(PASSES):
            nc.gpsimd.memset(scale[a][:].bitcast(I32), 0)
        v_s = [scale[a][:, 0:S] for a in range(PASSES)]
        w4_s = [scale[a][:, S : S + N] for a in range(PASSES)]
        w2_s = [scale[a][:, S + N : S + N + H] for a in range(PASSES)]
        gain_ps = psum.tile([P, P], F32, name="gain_ps")
        nc.tensor.transpose(gain_ps[:], gain_rows[:], ident[:])

        rows = held([P, S + N + H], U8, "rows")
        nc.vector.tensor_copy(rows[:, S : S + N].rearrange("p (t m) -> p t m", t=PACK),
                              w4s_raw[:].rearrange("p (m t) -> p t m", t=PACK))
        nc.vector.tensor_copy(rows[0:ROWS, S + N : S + N + H].bitcast(I32).rearrange("p (t q i) -> p t q i", t=PACK, i=2),
                              w2s_raw[:].rearrange("p (q t i) -> p t q i", t=PACK, i=2))
        v_w = [[held([P, HALF], U32, "v_w%d%d" % (a, b)) for b in range(2)] for a in range(PASSES)]
        v_sc = staged([P, S], U8, "v_sc", 32 * KB - S // 2)
        nc.vector.tensor_copy(v_sc[:], tab_sc[:].indirect(offs_sb[:]))
        nc.vector.tensor_copy(rows[0:ROWS, 0:S].bitcast(I32), v_sc[0:ROWS, :].bitcast(I32))

        def gather_words(a):
            for b in range(2):
                nc.vector.tensor_copy(v_w[a][b][:],
                                      tab_w[a][:].indirect(offs_sb[:, b * HALF // LANES : (b + 1) * HALF // LANES]))

        def move_scales(a):
            for q in range(QUADS):
                row = 16 * a + 4 * q
                nc.sync.dma_start(out=scale[a][32 * q : 32 * q + 4, :].bitcast(I32), in_=rows[row : row + 4, :].bitcast(I32))

        move_scales(0)
        load_tab(1)
        move_scales(1)
        w1_both = staged([P, PASSES, PACK, H], F32, "w1_both", 32 * KB)
        w1_raw = [w1_both[:, a] for a in range(PASSES)]
        for a in range(PASSES):
            nc.sync.dma_start(out=w1_raw[a], in_=w1[512 * a : 512 * (a + 1), :].rearrange("(p j) c -> p j c", j=PACK))
        gather_words(0)
        trust_sb = [staged([P, 2, S], F32, "trust_sb0", 0)]
        w3_raw = staged([P, PACK, N], F32, "w3_raw", 8 * KB)
        trust_rows = trust.rearrange("(p t) j -> p t j", t=PACK)
        nc.sync.dma_start(out=trust_sb[0][:], in_=trust_rows[:, 0:2, :])
        w3_rows = w3.rearrange("(q s i) n -> s q i n", s=PACK, i=8)
        for s in range(PACK):
            nc.sync.dma_start(out=w3_raw[:, s, :], in_=w3_rows[s])
        w4_q = held([P, PASSES * N], I32, "w4_q")
        nc.vector.tensor_copy(w4_q[:].rearrange("p (a t m i) -> p a m t i", a=PASSES, t=PACK, i=4),
                              w4_raw[:].rearrange("p (a m i t) -> p a m t i", a=PASSES, t=PACK, i=4))
        w2_q = held([P, PASSES * H * 2], U8, "w2_q")
        nc.vector.tensor_copy(w2_q[:].bitcast(I32).rearrange("p (a t q i) -> p a t q i", a=PASSES, t=PACK, i=4),
                              w2_raw[:].rearrange("p (a q t i) -> p a t q i", a=PASSES, t=PACK, i=4))
        gather_words(1)
        trust_sb.append(staged([P, 2, S], F32, "trust_sb1", 16 * KB))
        nc.sync.dma_start(out=trust_sb[1][:], in_=trust_rows[:, 2:PACK, :])

        skip = [held([P, S], F32, "skip%d" % t) for t in range(PACK)]

        def skip_product(b, ts):
            cols = slice(b * HALF, (b + 1) * HALF)
            banks = {t: psum.tile([P, HALF], F32, name="bank", bufs=BANKS) for t in ts}
            for a in range(PASSES):
                for t in ts:
                    nc.tensor.matmul_mx(out=banks[t][:], lhsT=w4_q[:, a * N + t * P : a * N + (t + 1) * P].bitcast(FP8X4),
                                        lhsT_scale=w4_s[a][:, t * P : (t + 1) * P],
                                        rhs=v_w[a][b][:].bitcast(FP8X4), rhs_scale=v_s[a][:, cols],
                                        start=(a == 0), stop=(a == PASSES - 1))
            for t in ts:
                nc.scalar.activation(out=skip[t][:, cols], in_=banks[t][:], func=ACT.Copy)

        skip_product(0, range(PACK))
        skip_product(1, range(2))
        skip_product(1, range(2, PACK))

        w1_q = {}
        w1_s = {}

        def quantise_w1(a, u):
            w1_q[a, u] = held([P, 2 * P], U32, "w1_q%d%d" % (a, u))
            w1_s[a, u] = held([P, 2 * P], U8, "w1_s%d%d" % (a, u))
            nc.vector.quantize_mx(out=w1_q[a, u][:].bitcast(FP8X4), scales=w1_s[a, u][:], in_=grouped[u][:])

        for a in range(PASSES):
            grouped = []
            for u in range(2):
                g = staged([P, 2 * P * PACK], BF16, "w1_g%d%d" % (a, u), (26, 48)[a] * KB + 2 * KB * u)
                for e in range(2):
                    nc.vector.tensor_copy(
                        g[:].rearrange("p (e q z i j) -> p e q z j i", e=2, z=2, i=4, j=PACK)[:, e],
                        w1_raw[a].rearrange("p j (q t z i) -> p t q z j i", t=PACK, z=2, i=4)[:, 2 * u + e])
                grouped.append(g)
                if a == 1:
                    quantise_w1(a, u)
            if a == 0:
                quantise_w1(a, 0)
                quantise_w1(a, 1)

        h_bf = [held([P, HALF * PACK], BF16, "h_bf%d" % b) for b in range(2)]
        h_q = [held([P, HALF], U32, "h_q%d" % b) for b in range(2)]
        h_s = [held([P, HALF], U8, "h_s%d" % b) for b in range(2)]
        w3_q = held([P, N], U32, "w3_q")
        w3_s = held([P, N], U8, "w3_s")
        gain_tn = gain_ps[:, 0:PACK].rearrange("p (u e) -> p u e", u=2).unsqueeze(1).to_broadcast([P, CHUNK, 2, 2])
        lesser = {}

        def products(c):
            cols = slice(c * CHUNK, (c + 1) * CHUNK)
            moving = [v_w[a][c // 2][:, (c % 2) * CHUNK : (c % 2 + 1) * CHUNK].bitcast(FP8X4) for a in range(PASSES)]
            lesser[c] = ring.tile([P, 2, CHUNK, 2], F32, name="lesser", align_bytes=64)
            for u in range(2):
                pre = psum.tile([P, 2, CHUNK], F32, name="bank", bufs=BANKS)
                for a in range(PASSES):
                    for e in range(2):
                        nc.tensor.matmul_mx(out=pre[:, e, :], lhsT=w1_q[a, u][:, e * P : (e + 1) * P].bitcast(FP8X4),
                                            lhsT_scale=w1_s[a, u][:, e * P : (e + 1) * P],
                                            rhs=moving[a], rhs_scale=v_s[a][:, cols],
                                            start=(a == 0 and e == 0), stop=(a == PASSES - 1 and e == 1))
                lin = psum.tile([P, 2, CHUNK], F32, name="bank", bufs=BANKS)
                for e in range(2):
                    t = 2 * u + e
                    for a in range(PASSES):
                        nc.tensor.matmul_mx(out=lin[:, e, :],
                                            lhsT=w2_q[:, 2 * (a * H + t * P) : 2 * (a * H + (t + 1) * P)].bitcast(FP4X4),
                                            lhsT_scale=w2_s[a][:, t * P : (t + 1) * P],
                                            rhs=moving[a], rhs_scale=v_s[a][:, cols],
                                            start=(a == 0), stop=(a == PASSES - 1))
                bounded = ring.tile([P, CHUNK, 2], F32, name="bounded", bufs=3)
                nc.scalar.activation(out=bounded[:], in_=pre[:].rearrange("p e n -> p n e"), func=ACT.Tanh)
                nc.vector.tensor_tensor(lesser[c][:, u], lin[:].rearrange("p e n -> p n e"), bounded[:], ALU.min)

        def apply_gain(c):
            dst = h_bf[c // 2][:, (c % 2) * CHUNK * PACK : (c % 2 + 1) * CHUNK * PACK]
            nc.vector.tensor_tensor(dst.rearrange("p (n u e) -> p n u e", u=2, e=2),
                                    lesser[c][:].rearrange("p u n e -> p n u e"), gain_tn, ALU.mult)

        def quantise_h(b):
            nc.vector.quantize_mx(out=h_q[b][:].bitcast(FP8X4), scales=h_s[b][:], in_=h_bf[b][:])

        def round_w3(part):
            ms = slice(32 * part, 32 * (part + 1))
            nc.scalar.activation(out=w3_g[:].rearrange("p (t m s) -> p m t s", t=PACK, s=PACK)[:, ms],
                                 in_=w3_raw[:].rearrange("p s (m t) -> p m t s", t=PACK)[:, ms], func=ACT.Copy)

        for t in range(PACK):
            for b in range(2):
                cols = slice(b * HALF, (b + 1) * HALF)
                nc.gpsimd.tensor_tensor(skip[t][:, cols], skip[t][:, cols], trust_sb[t // 2][:, t % 2, cols], ALU.mult)
        chunks = S // CHUNK
        for c in range(chunks):
            products(c)
            if c == 2:
                quantise_h(0)
                w3_g = ring.tile([P, N * PACK], BF16, name="w3_g", tag="lesser", align_bytes=64)
            apply_gain(c)
            if c >= 2:
                round_w3(2 * (c - 2))
                round_w3(2 * (c - 2) + 1)
        nc.vector.quantize_mx(out=w3_q[:].bitcast(FP8X4), scales=w3_s[:], in_=w3_g[:])
        quantise_h(1)

        g2 = [held([P, S], F32, "g2_%d" % t) for t in range(PACK)]
        y = held([P, PACK, M], F32, "y")
        y_rows = out_0.rearrange("(p t) m -> p t m", t=PACK)
        first = {}

        def second_stage(t, b):
            bank = psum.tile([P, HALF], F32, name="bank", bufs=BANKS)
            nc.tensor.matmul_mx(out=bank[:], lhsT=w3_q[:, t * P : (t + 1) * P].bitcast(FP8X4),
                                lhsT_scale=w3_s[:, t * P : (t + 1) * P],
                                rhs=h_q[b][:].bitcast(FP8X4), rhs_scale=h_s[b][:], start=True, stop=True)
            nc.vector.tensor_tensor(g2[t][:, b * HALF : (b + 1) * HALF], bank[:], skip[t][:, b * HALF : (b + 1) * HALF], ALU.subtract)

        def pick_first(t, lo, hi):
            first[t, lo] = ring.tile([P, M], F32, name="first", bufs=3)
            nc.vector.tensor_copy(first[t, lo][:, 0 : hi - lo], g2[t][:].indirect(pos1_sb[:, lo // LANES : hi // LANES]))

        def pick_second(t, lo, hi):
            diff = ring.tile([P, M], F32, name="diff", bufs=3)
            nc.vector.tensor_tensor(diff[:, 0 : hi - lo], g2[t][:].indirect(pos2_sb[:, lo // LANES : hi // LANES]),
                                    first[t, lo][:, 0 : hi - lo], ALU.subtract)
            nc.scalar.activation(out=y[:, t, lo:hi], in_=diff[:, 0 : hi - lo], func=ACT.Square)
            nc.sync.dma_start(out=y_rows[:, t, lo:hi], in_=y[:, t, lo:hi])

        y_q = held([P, M], U32, "y_q")
        y_s = held([P, M], U8, "y_s")
        y_bf = [held([P, M // 2 * PACK], BF16, "y_bf%d" % b) for b in range(2)]
        words_out = out_1[0].rearrange("p m t -> p (m t)").bitcast(I32)
        mid = M // 2

        def planes(b):
            cols = slice(b * mid, (b + 1) * mid)
            nc.vector.quantize_mx(out=y_q[:, cols].bitcast(FP8X4), scales=y_s[:, cols], in_=y_bf[b][:])
            nc.sync.dma_start(out=words_out[:, cols], in_=y_q[:, cols].bitcast(I32))

        def y_views(b):
            return (y_bf[b][:].rearrange("p (c i t) -> p c t i", i=4, t=PACK),
                    y[:, :, b * mid : (b + 1) * mid].rearrange("p t (c i) -> p c t i", i=4))

        second_stage(0, 0)
        second_stage(1, 0)
        second_stage(0, 1)
        for t in range(2):
            second_stage(t + 2, 0)
            pick_first(t, 0, M)
            second_stage(t + 1, 1)
            pick_second(t, 0, M)
        pick_first(2, 0, mid)
        second_stage(3, 1)
        pick_second(2, 0, mid)
        pick_first(3, 0, mid)
        pick_first(2, mid, M)
        pick_second(3, 0, mid)
        dst, src = y_views(0)
        nc.scalar.activation(out=dst, in_=src, func=ACT.Copy)
        pick_first(3, mid, M)
        pick_second(2, mid, M)
        pick_second(3, mid, M)
        planes(0)
        dst, src = y_views(1)
        nc.vector.tensor_copy(dst, src)
        planes(1)
        for q in range(QUADS):
            eng = (nc.sync, nc.scalar)[q % 2]
            eng.dma_start(out=out_2[0, 4 * q : 4 * q + 4, :].bitcast(I32), in_=y_s[32 * q : 32 * q + 4, :].bitcast(I32))
